import numpy as np
import ml_dtypes


def mxq(x, axis, fmt="e4m3"):
    dtype, down = {"e4m3": (ml_dtypes.float8_e4m3fn, 7), "e5m2": (ml_dtypes.float8_e5m2, 14)}[fmt]
    v = np.moveaxis(np.asarray(x, np.float32).astype(ml_dtypes.bfloat16).astype(np.float64), axis, -1)
    blocks = v.reshape(v.shape[:-1] + (-1, 32))
    amax = np.abs(blocks).max(-1, keepdims=True)
    byte = np.maximum(np.where(amax > 0, np.frexp(amax)[1] - 1 + 127, 0) - down, 1)
    scale = np.exp2(byte - 127.0)
    codes = (blocks / scale).astype(np.float32).astype(dtype).astype(np.float64)
    return np.moveaxis((codes * scale).reshape(v.shape), -1, axis)


WIDE = False


def mx_kscale(k, group=512):
    if not WIDE:
        return np.ones(k)
    levels = np.array([10, -10, 5, -5, 0])
    if group != 512:
        return np.exp2(np.random.permutation(np.resize(levels, k // group))).repeat(group)
    if k % 512:
        return np.exp2(np.random.permutation(np.resize(levels, k // 32))).repeat(32)
    a = np.empty((k // 512, 16))
    for p in range(k // 512):
        a[p, :8] = np.random.permutation(np.resize(levels, 8))
        for g in range(8):
            far = levels[np.abs(levels - a[p, g]) >= 10]
            a[p, g + 8] = far[np.random.randint(len(far))]
    return np.exp2(a.ravel()).repeat(32)


def f64(x):
    return np.asarray(x).astype(np.float64)


def sigmoid(v):
    return 1.0 / (1.0 + np.exp(-v))


def bf(x):
    return np.asarray(x, np.float32).astype(ml_dtypes.bfloat16)


def planes(Y):
    r, m = Y.shape
    b = f64(bf(Y)).reshape(r // 32, 32, m)
    amax = np.abs(b).max(1)
    byte = np.clip(np.where(amax > 0, np.frexp(amax)[1] - 1 + 127 - 7, 1), 1, 254)
    codes = (b * np.exp2(127.0 - byte)[:, None, :]).reshape(r, m).astype(np.float32).astype(ml_dtypes.float8_e4m3fn).view(np.uint8)
    words = codes.reshape(r // 512, 128, 4, m).transpose(0, 1, 3, 2)
    return np.ascontiguousarray(words), np.ascontiguousarray(byte.astype(np.uint8).reshape(r // 512, 16, m))


G, D, M, N = 2, 256, 256, 512


def setup_inputs():
    n = np.random.standard_normal
    s_d = mx_kscale(D, 0)
    return {
        "h": (n((G, D, N)) * s_d[:, None]).astype(np.float32),
        "wr": (n((G, D, M)) / np.sqrt(D) / s_d[:, None]).astype(np.float32),
        "wi": (n((G, D, M)) / np.sqrt(D) / s_d[:, None]).astype(np.float32),
        "xh": (n((G, M, N))).astype(np.float32),
        "hp": (n((G, M, N))).astype(np.float32),
        "la": (-np.random.uniform(0.3, 3.0, (G, M, 1))).astype(np.float32),
        "br": (0.5 * n((G, M, 1))).astype(np.float32),
        "bi": (0.5 * n((G, M, 1))).astype(np.float32),
    }


def reference(h, wr, wi, xh, hp, la, br, bi):
    wrq = mxq(f64(wr), 1, "e4m3")
    hq = mxq(f64(h), 1, "e4m3")
    zr = wrq.transpose(0, 2, 1) @ hq
    wiq = mxq(f64(wi), 1, "e4m3")
    zi = wiq.transpose(0, 2, 1) @ hq
    a = np.exp(f64(la) * sigmoid(zr + f64(br)))
    y = a * f64(hp) + np.sqrt(1.0 - a * a) * sigmoid(zi + f64(bi)) * f64(xh)
    Y = y.reshape(G * M, N)
    words, scales = planes(Y)
    return Y, words, scales

@@ -1,0 +1,192 @@
+from contextlib import ExitStack
+
+import concourse.mybir as mybir
+
+G, D, M, N = 2, 256, 256, 512
+FLOPS = 2 * G * 2 * D * M * N
+
+F32 = mybir.dt.float32
+BF16 = mybir.dt.bfloat16
+I32 = mybir.dt.int32
+U32 = mybir.dt.uint32
+U8 = mybir.dt.uint8
+FP8X4 = mybir.dt.float8_e4m3fn_x4
+ACT = mybir.ActivationFunctionType
+ALU = mybir.AluOpType
+
+P = 128
+PACK = 4
+ROWS = D // PACK
+PAIR = M // P
+H_SPLIT = 344
+CHUNKS = [(0, 256), (256, 128), (384, 128)]
+
+
+def tile_rows_pl_cell_rglru_kernel(tc, h, wr, wi, xh, hp, la, br, bi, out_0, out_1, out_2):
+    nc = tc.nc
+    with ExitStack() as ctx:
+        sb = ctx.enter_context(tc.tile_pool(name="sb", bufs=1))
+        psum = ctx.enter_context(tc.psum_pool(name="psum", bufs=1))
+        ctx.enter_context(tc.manual_schedule())
+
+        def new(name, shape, dtype):
+            return sb.tile(shape, dtype, name=name, align_bytes=64)
+
+        par = new("par", [P, 3, 8], F32)
+        for k, vec in enumerate((br, la, bi)):
+            nc.scalar.dma_start(
+                out=par[:, k, 0:4].rearrange("q (g j) -> q g j", j=PAIR),
+                in_=vec.rearrange("g (q j) o -> q g (j o)", j=PAIR),
+            )
+        h_raw = new("h_raw", [P, PACK, N], F32)
+        nc.sync.dma_start(out=h_raw[:], in_=h.rearrange("g (p t) n -> (g p) t n", t=PACK))
+        w_raw = []
+        for k, w in enumerate((wr, wi)):
+            w_raw.append(new("w_raw%d" % k, [P, PACK, M], F32))
+            nc.sync.dma_start(out=w_raw[k][:], in_=w.rearrange("g (p t) m -> (g p) t m", t=PACK))
+        hp_sb, xh_sb = [], []
+        for name, src, dst in (("hp", hp, hp_sb), ("xh", xh, xh_sb)):
+            for g in range(G):
+                dst.append(new("%s%d" % (name, g), [P, PAIR, N], F32))
+                nc.sync.dma_start(out=dst[g][:], in_=src[g].rearrange("(q j) n -> q j n", j=PAIR))
+
+        half = new("half", [P, 3, 4], F32)
+        nc.gpsimd.tensor_scalar(out=half[:], in0=par[:, :, 0:4], scalar1=0.5, scalar2=0.0, op0=ALU.mult, op1=ALU.add)
+
+        def col(k, g, j):
+            return half[:, k, PAIR * g + j : PAIR * g + j + 1]
+
+        h_bf = new("h_bf", [P, N, PACK], BF16)
+        h_in = h_raw[:].rearrange("p t n -> p n t")
+        nc.vector.tensor_copy(out=h_bf[:, :H_SPLIT, :], in_=h_in[:, :H_SPLIT, :])
+        nc.scalar.copy(out=h_bf[:, H_SPLIT:, :], in_=h_in[:, H_SPLIT:, :])
+        h_codes = new("h_codes", [P, N], U32)
+        h_scales = new("h_scales", [P, N], U8)
+        nc.vector.quantize_mx(out=h_codes[:].bitcast(FP8X4), scales=h_scales[:], in_=h_bf[:].rearrange("p n t -> p (n t)"))
+
+        w_bf, w_codes, w_scales = {}, {}, {}
+
+        def round_w(k, j, copy):
+            w_bf[k, j] = new("w_bf%d%d" % (k, j), [P, P, PACK], BF16)
+            copy(out=w_bf[k, j][:], in_=w_raw[k][:].rearrange("p t (q j) -> p j q t", j=PAIR)[:, j])
+
+        def quant_w(k, j):
+            w_codes[k, j] = new("w_codes%d%d" % (k, j), [P, P], U32)
+            w_scales[k, j] = new("w_scales%d%d" % (k, j), [P, P], U8)
+            nc.vector.quantize_mx(
+                out=w_codes[k, j][:].bitcast(FP8X4),
+                scales=w_scales[k, j][:],
+                in_=w_bf[k, j][:].rearrange("p q t -> p (q t)"),
+            )
+
+        z = {}
+
+        def product(k, g, j):
+            z[k, g, j] = psum.tile([P, N], F32, name="z%d%d%d" % (k, g, j))
+            rows = slice(ROWS * g, ROWS * (g + 1))
+            nc.tensor.matmul_mx(
+                out=z[k, g, j][:],
+                lhsT=w_codes[k, j][rows, :].bitcast(FP8X4),
+                lhsT_scale=w_scales[k, j][rows, :],
+                rhs=h_codes[rows, :].bitcast(FP8X4),
+                rhs_scale=h_scales[rows, :],
+                start=True,
+                stop=True,
+            )
+
+        round_w(0, 0, nc.scalar.copy)
+        round_w(0, 1, nc.vector.tensor_copy)
+        quant_w(0, 0)
+        quant_w(0, 1)
+        round_w(1, 0, nc.vector.tensor_copy)
+        round_w(1, 1, nc.vector.tensor_copy)
+        quant_w(1, 0)
+        quant_w(1, 1)
+        for k in range(2):
+            for g in range(G):
+                for j in range(PAIR):
+                    product(k, g, j)
+
+        tr, a, a2, u, ti, v = [], [], [], [], [], []
+        for g in range(G):
+            tr.append(new("tr%d" % g, [P, PAIR, N], F32))
+            a.append(new("a%d" % g, [P, PAIR, N], F32))
+            a2.append(new("a2%d" % g, [P, PAIR, N], F32))
+            u.append(new("u%d" % g, [P, PAIR, N], F32))
+            for j in range(PAIR):
+                nc.scalar.activation(out=tr[g][:, j, :], in_=z[0, g, j][:], func=ACT.Tanh, bias=col(0, g, j), scale=0.5)
+            for j in range(PAIR):
+                nc.scalar.activation(out=a[g][:, j, :], in_=tr[g][:, j, :], func=ACT.Exp, bias=col(1, g, j), scale=col(1, g, j))
+            for j in range(PAIR):
+                nc.vector.tensor_tensor(out=a2[g][:, j, :], in0=a[g][:, j, :], in1=a[g][:, j, :], op=ALU.mult)
+                nc.vector.tensor_tensor(out=u[g][:, j, :], in0=a[g][:, j, :], in1=hp_sb[g][:, j, :], op=ALU.mult)
+        for g in range(G):
+            ti.append(new("ti%d" % g, [P, PAIR, N], F32))
+            v.append(new("v%d" % g, [P, PAIR, N], F32))
+            for j in range(PAIR):
+                nc.scalar.activation(out=ti[g][:, j, :], in_=z[1, g, j][:], func=ACT.Tanh, bias=col(2, g, j), scale=0.5)
+            for j in range(PAIR):
+                nc.vector.scalar_tensor_tensor(
+                    out=v[g][:, j, :], in0=ti[g][:, j, :], scalar=1.0, in1=xh_sb[g][:, j, :], op0=ALU.add, op1=ALU.mult
+                )
+
+        pieces = [(0, c) for c in reversed(range(len(CHUNKS)))] + [(1, c) for c in range(len(CHUNKS))]
+        y = [new("y%d" % g, [P, PAIR, N], F32) for g in range(G)]
+        s, m, moved = {}, {}, {}
+        for c, (n0, w) in enumerate(CHUNKS):
+            moved[c] = new("moved%d" % c, [P, 2, w], F32)
+
+        def cols(c):
+            return slice(CHUNKS[c][0], CHUNKS[c][0] + CHUNKS[c][1])
+
+        def root(g, c):
+            s[g, c] = new("s%d%d" % (g, c), [P, PAIR, CHUNKS[c][1]], F32)
+            nc.scalar.activation(out=s[g, c][:], in_=a2[g][:, :, cols(c)], func=ACT.Sqrt, bias=0.25, scale=-0.25)
+
+        def scale_in(g, c):
+            m[g, c] = new("m%d%d" % (g, c), [P, PAIR, CHUNKS[c][1]], F32)
+            nc.vector.tensor_tensor(out=m[g, c][:], in0=s[g, c][:], in1=v[g][:, :, cols(c)], op=ALU.mult)
+
+        def add(g, c):
+            nc.vector.tensor_tensor(out=y[g][:, :, cols(c)], in0=m[g, c][:], in1=u[g][:, :, cols(c)], op=ALU.add)
+
+        def round_and_move(g, c):
+            pairs = new("pairs%d%d" % (g, c), [P, CHUNKS[c][1], PAIR], BF16)
+            nc.scalar.copy(out=pairs[:], in_=y[g][:, :, cols(c)].rearrange("q j n -> q n j"))
+            nc.sync.dma_start(
+                out=moved[c][ROWS * g : ROWS * (g + 1), :, :],
+                in_=pairs[:].rearrange("q n j -> q (n j)").bitcast(F32),
+            )
+
+        def store_y(g, columns):
+            rows = out_0[M * g : M * (g + 1), :].rearrange("(q j) n -> q j n", j=PAIR)
+            nc.sync.dma_start(out=rows[:, :, columns], in_=y[g][:, :, columns])
+
+        for g, c in pieces:
+            root(g, c)
+        scale_in(*pieces[0])
+        for i, (g, c) in enumerate(pieces):
+            if i + 1 < len(pieces):
+                scale_in(*pieces[i + 1])
+            add(g, c)
+            if i == 2:
+                store_y(0, slice(0, N))
+            if i == 3:
+                store_y(1, cols(0))
+            round_and_move(g, c)
+        store_y(1, slice(CHUNKS[1][0], N))
+
+        y_codes = new("y_codes", [P, N], U32)
+        y_scales = new("y_scales", [P, N], U8)
+        words = out_1[0].rearrange("p n t -> p (n t)").bitcast(I32)
+        for c, (n0, w) in enumerate(CHUNKS):
+            y_bf = new("y_bf%d" % c, [P, w * PACK], BF16)
+            nc.vector.tensor_copy(
+                out=y_bf[:].bitcast(F32).rearrange("p (n a) -> p n a", a=2),
+                in_=moved[c][:].rearrange("p a n -> p n a"),
+            )
+            nc.vector.quantize_mx(out=y_codes[:, cols(c)].bitcast(FP8X4), scales=y_scales[:, cols(c)], in_=y_bf[:])
+            nc.sync.dma_start(out=words[:, cols(c)], in_=y_codes[:, cols(c)].bitcast(I32))
+        for q in range(4):
+            queue = nc.scalar if q % 2 else nc.sync
+            queue.dma_start(out=out_2[0, 4 * q : 4 * q + 4, :].bitcast(I32), in_=y_scales[32 * q : 32 * q + 4, :].bitcast(I32))

@@ -32,14 +32,12 @@ def tile_rows_pl_cell_rglru_kernel(tc, h, wr, wi, xh, hp, la, br, bi, out_0, out
         def new(name, shape, dtype):
             return sb.tile(shape, dtype, name=name, align_bytes=64)
 
-        par = new("par", [P, 3, 8], F32)
-        for k, vec in enumerate((br, la, bi)):
-            nc.scalar.dma_start(
-                out=par[:, k, 0:4].rearrange("q (g j) -> q g j", j=PAIR),
-                in_=vec.rearrange("g (q j) o -> q g (j o)", j=PAIR),
-            )
+        par = new("par", [P, G, 64], F32)
+        nc.vector.memset(par[:], 0.0)
         h_raw = new("h_raw", [P, PACK, N], F32)
         nc.sync.dma_start(out=h_raw[:], in_=h.rearrange("g (p t) n -> (g p) t n", t=PACK))
+        for k, vec in enumerate((br, la, bi)):
+            nc.sync.dma_start(out=par[k:P:32, :, :], in_=vec.rearrange("g (b x) o -> b g (x o)", x=64))
         w_raw = []
         for k, w in enumerate((wr, wi)):
             w_raw.append(new("w_raw%d" % k, [P, PACK, M], F32))
@@ -50,16 +48,15 @@ def tile_rows_pl_cell_rglru_kernel(tc, h, wr, wi, xh, hp, la, br, bi, out_0, out
                 dst.append(new("%s%d" % (name, g), [P, PAIR, N], F32))
                 nc.sync.dma_start(out=dst[g][:], in_=src[g].rearrange("(q j) n -> q j n", j=PAIR))
 
-        half = new("half", [P, 3, 4], F32)
-        nc.gpsimd.tensor_scalar(out=half[:], in0=par[:, :, 0:4], scalar1=0.5, scalar2=0.0, op0=ALU.mult, op1=ALU.add)
-
         def col(k, g, j):
-            return half[:, k, PAIR * g + j : PAIR * g + j + 1]
+            x = 32 * (PAIR * g + j) + k
+            return half[:, x : x + 1]
 
         h_bf = new("h_bf", [P, N, PACK], BF16)
-        h_in = h_raw[:].rearrange("p t n -> p n t")
-        nc.vector.tensor_copy(out=h_bf[:, :H_SPLIT, :], in_=h_in[:, :H_SPLIT, :])
-        nc.scalar.copy(out=h_bf[:, H_SPLIT:, :], in_=h_in[:, H_SPLIT:, :])
+        h_in = h_raw[:].rearrange("p t (c i) -> p c t i", i=4)
+        h_out = h_bf[:].rearrange("p (c i) t -> p c t i", i=4)
+        nc.vector.tensor_copy(out=h_out[:, : H_SPLIT // 4], in_=h_in[:, : H_SPLIT // 4])
+        nc.scalar.copy(out=h_out[:, H_SPLIT // 4 :], in_=h_in[:, H_SPLIT // 4 :])
         h_codes = new("h_codes", [P, N], U32)
         h_scales = new("h_scales", [P, N], U8)
         nc.vector.quantize_mx(out=h_codes[:].bitcast(FP8X4), scales=h_scales[:], in_=h_bf[:].rearrange("p n t -> p (n t)"))
@@ -68,7 +65,10 @@ def tile_rows_pl_cell_rglru_kernel(tc, h, wr, wi, xh, hp, la, br, bi, out_0, out
 
         def round_w(k, j, copy):
             w_bf[k, j] = new("w_bf%d%d" % (k, j), [P, P, PACK], BF16)
-            copy(out=w_bf[k, j][:], in_=w_raw[k][:].rearrange("p t (q j) -> p j q t", j=PAIR)[:, j])
+            copy(
+                out=w_bf[k, j][:].rearrange("p (c i) t -> p c t i", i=2),
+                in_=w_raw[k][:].rearrange("p t (c i j) -> p j c t i", i=2, j=PAIR)[:, j],
+            )
 
         def quant_w(k, j):
             w_codes[k, j] = new("w_codes%d%d" % (k, j), [P, P], U32)
@@ -98,6 +98,17 @@ def tile_rows_pl_cell_rglru_kernel(tc, h, wr, wi, xh, hp, la, br, bi, out_0, out
         round_w(0, 1, nc.vector.tensor_copy)
         quant_w(0, 0)
         quant_w(0, 1)
+        halved = new("halved", [P, G * PAIR * 32], F32)
+        nc.vector.tensor_scalar(
+            out=halved[:].rearrange("r (g j a) -> r g j a", g=G, j=PAIR),
+            in0=par[:].rearrange("r g (a j) -> r g j a", j=PAIR),
+            scalar1=0.5,
+            scalar2=None,
+            op0=ALU.mult,
+        )
+        half = new("half", [P, G * PAIR * 32], F32)
+        nc.vector.transpose(out=half[:], in_=halved[:])
+
         round_w(1, 0, nc.vector.tensor_copy)
         round_w(1, 1, nc.vector.tensor_copy)
         quant_w(1, 0)
@@ -169,12 +180,9 @@ def tile_rows_pl_cell_rglru_kernel(tc, h, wr, wi, xh, hp, la, br, bi, out_0, out
             if i + 1 < len(pieces):
                 scale_in(*pieces[i + 1])
             add(g, c)
-            if i == 2:
-                store_y(0, slice(0, N))
-            if i == 3:
-                store_y(1, cols(0))
             round_and_move(g, c)
-        store_y(1, slice(CHUNKS[1][0], N))
+            if i % len(CHUNKS) == len(CHUNKS) - 1:
+                store_y(g, slice(0, N))
 
         y_codes = new("y_codes", [P, N], U32)
         y_scales = new("y_scales", [P, N], U8)

@@ -18,8 +18,10 @@ P = 128
 PACK = 4
 ROWS = D // PACK
 PAIR = M // P
-H_SPLIT = 344
-CHUNKS = [(0, 256), (256, 128), (384, 128)]
+HALF = N // 2
+STEP = 128
+H_SPLIT = 176
+CHUNKS = [(0, 128), (128, 256), (384, 128)]
 
 
 def tile_rows_pl_cell_rglru_kernel(tc, h, wr, wi, xh, hp, la, br, bi, out_0, out_1, out_2):
@@ -34,14 +36,23 @@ def tile_rows_pl_cell_rglru_kernel(tc, h, wr, wi, xh, hp, la, br, bi, out_0, out
 
         par = new("par", [P, G, 64], F32)
         nc.vector.memset(par[:], 0.0)
-        h_raw = new("h_raw", [P, PACK, N], F32)
-        nc.sync.dma_start(out=h_raw[:], in_=h.rearrange("g (p t) n -> (g p) t n", t=PACK))
+
+        def load_w(k, w):
+            raw = new("w_raw%d" % k, [P, PACK, M], F32)
+            nc.sync.dma_start(out=raw[:], in_=w.rearrange("g (p t) m -> (g p) t m", t=PACK))
+            return raw
+
+        def load_h(e):
+            raw = new("h_raw%d" % e, [P, PACK, HALF], F32)
+            nc.sync.dma_start(out=raw[:], in_=h.rearrange("g (p t) n -> (g p) t n", t=PACK)[:, :, HALF * e : HALF * (e + 1)])
+            return raw
+
+        h_raw = [load_h(0)]
         for k, vec in enumerate((br, la, bi)):
             nc.sync.dma_start(out=par[k:P:32, :, :], in_=vec.rearrange("g (b x) o -> b g (x o)", x=64))
-        w_raw = []
-        for k, w in enumerate((wr, wi)):
-            w_raw.append(new("w_raw%d" % k, [P, PACK, M], F32))
-            nc.sync.dma_start(out=w_raw[k][:], in_=w.rearrange("g (p t) m -> (g p) t m", t=PACK))
+        w_raw = [load_w(0, wr)]
+        h_raw.append(load_h(1))
+        w_raw.append(load_w(1, wi))
         hp_sb, xh_sb = [], []
         for name, src, dst in (("hp", hp, hp_sb), ("xh", xh, xh_sb)):
             for g in range(G):
@@ -52,137 +63,168 @@ def tile_rows_pl_cell_rglru_kernel(tc, h, wr, wi, xh, hp, la, br, bi, out_0, out
             x = 32 * (PAIR * g + j) + k
             return half[:, x : x + 1]
 
-        h_bf = new("h_bf", [P, N, PACK], BF16)
-        h_in = h_raw[:].rearrange("p t (c i) -> p c t i", i=4)
-        h_out = h_bf[:].rearrange("p (c i) t -> p c t i", i=4)
-        nc.vector.tensor_copy(out=h_out[:, : H_SPLIT // 4], in_=h_in[:, : H_SPLIT // 4])
-        nc.scalar.copy(out=h_out[:, H_SPLIT // 4 :], in_=h_in[:, H_SPLIT // 4 :])
-        h_codes = new("h_codes", [P, N], U32)
-        h_scales = new("h_scales", [P, N], U8)
-        nc.vector.quantize_mx(out=h_codes[:].bitcast(FP8X4), scales=h_scales[:], in_=h_bf[:].rearrange("p n t -> p (n t)"))
+        h_bf, h_codes, h_scales = {}, {}, {}
 
-        w_bf, w_codes, w_scales = {}, {}, {}
+        def round_h(e, split):
+            h_bf[e] = new("h_bf%d" % e, [P, HALF, PACK], BF16)
+            h_in = h_raw[e][:].rearrange("p t (c i) -> p c t i", i=4)
+            h_out = h_bf[e][:].rearrange("p (c i) t -> p c t i", i=4)
+            nc.vector.tensor_copy(out=h_out[:, : split // 4], in_=h_in[:, : split // 4])
+            if split < HALF:
+                nc.scalar.copy(out=h_out[:, split // 4 :], in_=h_in[:, split // 4 :])
 
-        def round_w(k, j, copy):
-            w_bf[k, j] = new("w_bf%d%d" % (k, j), [P, P, PACK], BF16)
-            copy(
-                out=w_bf[k, j][:].rearrange("p (c i) t -> p c t i", i=2),
-                in_=w_raw[k][:].rearrange("p t (c i j) -> p j c t i", i=2, j=PAIR)[:, j],
+        def quant_h(e):
+            h_codes[e] = new("h_codes%d" % e, [P, HALF], U32)
+            h_scales[e] = new("h_scales%d" % e, [P, HALF], U8)
+            nc.vector.quantize_mx(
+                out=h_codes[e][:].bitcast(FP8X4), scales=h_scales[e][:], in_=h_bf[e][:].rearrange("p n t -> p (n t)")
             )
 
-        def quant_w(k, j):
-            w_codes[k, j] = new("w_codes%d%d" % (k, j), [P, P], U32)
-            w_scales[k, j] = new("w_scales%d%d" % (k, j), [P, P], U8)
+        w_bf = [new("w_bf%d" % k, [P, PAIR, P, PACK], BF16) for k in range(2)]
+        w_codes = [new("w_codes%d" % k, [P, PAIR * P], U32) for k in range(2)]
+        w_scales = [new("w_scales%d" % k, [P, PAIR * P], U8) for k in range(2)]
+
+        def round_w(k, js, copy):
+            copy(
+                out=w_bf[k][:].rearrange("p j (c i) t -> p c t i j", i=2)[:, :, :, :, js],
+                in_=w_raw[k][:].rearrange("p t (c i j) -> p c t i j", i=2, j=PAIR)[:, :, :, :, js],
+            )
+
+        def quant_w(k, js):
+            part = slice(P * js.start, P * js.stop)
             nc.vector.quantize_mx(
-                out=w_codes[k, j][:].bitcast(FP8X4),
-                scales=w_scales[k, j][:],
-                in_=w_bf[k, j][:].rearrange("p q t -> p (q t)"),
+                out=w_codes[k][:, part].bitcast(FP8X4),
+                scales=w_scales[k][:, part],
+                in_=w_bf[k][:, js].rearrange("p j q t -> p (j q t)"),
             )
 
         z = {}
-
-        def product(k, g, j):
-            z[k, g, j] = psum.tile([P, N], F32, name="z%d%d%d" % (k, g, j))
-            rows = slice(ROWS * g, ROWS * (g + 1))
-            nc.tensor.matmul_mx(
-                out=z[k, g, j][:],
-                lhsT=w_codes[k, j][rows, :].bitcast(FP8X4),
-                lhsT_scale=w_scales[k, j][rows, :],
-                rhs=h_codes[rows, :].bitcast(FP8X4),
-                rhs_scale=h_scales[rows, :],
-                start=True,
-                stop=True,
-            )
-
-        round_w(0, 0, nc.scalar.copy)
-        round_w(0, 1, nc.vector.tensor_copy)
-        quant_w(0, 0)
-        quant_w(0, 1)
-        halved = new("halved", [P, G * PAIR * 32], F32)
-        nc.vector.tensor_scalar(
-            out=halved[:].rearrange("r (g j a) -> r g j a", g=G, j=PAIR),
-            in0=par[:].rearrange("r g (a j) -> r g j a", j=PAIR),
-            scalar1=0.5,
-            scalar2=None,
-            op0=ALU.mult,
-        )
-        half = new("half", [P, G * PAIR * 32], F32)
-        nc.vector.transpose(out=half[:], in_=halved[:])
-
-        round_w(1, 0, nc.vector.tensor_copy)
-        round_w(1, 1, nc.vector.tensor_copy)
-        quant_w(1, 0)
-        quant_w(1, 1)
         for k in range(2):
             for g in range(G):
                 for j in range(PAIR):
-                    product(k, g, j)
+                    z[k, g, j] = psum.tile([P, N], F32, name="z%d%d%d" % (k, g, j))
 
-        tr, a, a2, u, ti, v = [], [], [], [], [], []
+        def products(k, j, e):
+            for n0 in range(0, HALF, STEP):
+                for g in range(G):
+                    rows = slice(ROWS * g, ROWS * (g + 1))
+                    nc.tensor.matmul_mx(
+                        out=z[k, g, j][:, HALF * e + n0 : HALF * e + n0 + STEP],
+                        lhsT=w_codes[k][rows, P * j : P * (j + 1)].bitcast(FP8X4),
+                        lhsT_scale=w_scales[k][rows, P * j : P * (j + 1)],
+                        rhs=h_codes[e][rows, n0 : n0 + STEP].bitcast(FP8X4),
+                        rhs_scale=h_scales[e][rows, n0 : n0 + STEP],
+                        start=True,
+                        stop=True,
+                    )
+
+        round_h(0, H_SPLIT)
+        halved = new("halved", [P, G * PAIR * 32], F32)
+        nc.scalar.activation(
+            out=halved[:].rearrange("r (g j a) -> r g j a", g=G, j=PAIR),
+            in_=par[:].rearrange("r g (a j) -> r g j a", j=PAIR),
+            func=ACT.Copy,
+            scale=0.5,
+        )
+        quant_h(0)
+        half = new("half", [P, G * PAIR * 32], F32)
+        nc.vector.transpose(out=half[:], in_=halved[:])
+        round_w(0, slice(0, 1), nc.vector.tensor_copy)
+        round_w(0, slice(1, 2), nc.scalar.copy)
+        quant_w(0, slice(0, 1))
+        quant_w(0, slice(1, 2))
+        round_h(1, HALF)
+        quant_h(1)
+        round_w(1, slice(0, 2), nc.vector.tensor_copy)
+        quant_w(1, slice(0, 2))
+
+        tr, a, u, ti, v = [], [], [], [], []
+        a2 = new("a2", [P, G, PAIR, N], F32)
         for g in range(G):
             tr.append(new("tr%d" % g, [P, PAIR, N], F32))
             a.append(new("a%d" % g, [P, PAIR, N], F32))
-            a2.append(new("a2%d" % g, [P, PAIR, N], F32))
             u.append(new("u%d" % g, [P, PAIR, N], F32))
+
+        def tanh_r(g, j, e):
+            part = slice(HALF * e, HALF * (e + 1))
+            nc.scalar.activation(out=tr[g][:, j, part], in_=z[0, g, j][:, part], func=ACT.Tanh, bias=col(0, g, j), scale=0.5)
+
+        for j in range(PAIR):
+            products(0, j, 0)
+        for j in range(PAIR):
+            for g in range(G):
+                tanh_r(g, j, 0)
+        for j in range(PAIR):
+            products(0, j, 1)
+        for j in range(PAIR):
+            for e in range(2):
+                products(1, j, e)
+        for g in range(G):
             for j in range(PAIR):
-                nc.scalar.activation(out=tr[g][:, j, :], in_=z[0, g, j][:], func=ACT.Tanh, bias=col(0, g, j), scale=0.5)
+                tanh_r(g, j, 1)
             for j in range(PAIR):
                 nc.scalar.activation(out=a[g][:, j, :], in_=tr[g][:, j, :], func=ACT.Exp, bias=col(1, g, j), scale=col(1, g, j))
-            for j in range(PAIR):
-                nc.vector.tensor_tensor(out=a2[g][:, j, :], in0=a[g][:, j, :], in1=a[g][:, j, :], op=ALU.mult)
-                nc.vector.tensor_tensor(out=u[g][:, j, :], in0=a[g][:, j, :], in1=hp_sb[g][:, j, :], op=ALU.mult)
+            for js in [slice(0, 1), slice(1, 2)] if g == 0 else [slice(0, 2)]:
+                nc.vector.tensor_tensor(out=a2[:, g, js, :], in0=a[g][:, js, :], in1=a[g][:, js, :], op=ALU.mult)
+                nc.vector.tensor_tensor(out=u[g][:, js, :], in0=a[g][:, js, :], in1=hp_sb[g][:, js, :], op=ALU.mult)
         for g in range(G):
             ti.append(new("ti%d" % g, [P, PAIR, N], F32))
             v.append(new("v%d" % g, [P, PAIR, N], F32))
             for j in range(PAIR):
                 nc.scalar.activation(out=ti[g][:, j, :], in_=z[1, g, j][:], func=ACT.Tanh, bias=col(2, g, j), scale=0.5)
-            for j in range(PAIR):
-                nc.vector.scalar_tensor_tensor(
-                    out=v[g][:, j, :], in0=ti[g][:, j, :], scalar=1.0, in1=xh_sb[g][:, j, :], op0=ALU.add, op1=ALU.mult
-                )
+            nc.vector.scalar_tensor_tensor(out=v[g][:], in0=ti[g][:], scalar=1.0, in1=xh_sb[g][:], op0=ALU.add, op1=ALU.mult)
 
-        pieces = [(0, c) for c in reversed(range(len(CHUNKS)))] + [(1, c) for c in range(len(CHUNKS))]
-        y = [new("y%d" % g, [P, PAIR, N], F32) for g in range(G)]
-        s, m, moved = {}, {}, {}
+        pieces = [(g, c) for c in range(len(CHUNKS)) for g in range(G)]
+        y = new("y", [P, G, PAIR, N], F32)
+        s, m, pairs, moved = [], [], [], []
         for c, (n0, w) in enumerate(CHUNKS):
-            moved[c] = new("moved%d" % c, [P, 2, w], F32)
+            s.append(new("s%d" % c, [P, G, PAIR, w], F32))
+            m.append(new("m%d" % c, [P, G, PAIR, w], F32))
+            pairs.append(new("pairs%d" % c, [P, G, w, PAIR], BF16))
+            moved.append(new("moved%d" % c, [P, 2, w], F32))
 
         def cols(c):
             return slice(CHUNKS[c][0], CHUNKS[c][0] + CHUNKS[c][1])
 
-        def root(g, c):
-            s[g, c] = new("s%d%d" % (g, c), [P, PAIR, CHUNKS[c][1]], F32)
-            nc.scalar.activation(out=s[g, c][:], in_=a2[g][:, :, cols(c)], func=ACT.Sqrt, bias=0.25, scale=-0.25)
+        def root(gs, c):
+            nc.scalar.activation(out=s[c][:, gs], in_=a2[:, gs, :, cols(c)], func=ACT.Sqrt, bias=0.25, scale=-0.25)
 
         def scale_in(g, c):
-            m[g, c] = new("m%d%d" % (g, c), [P, PAIR, CHUNKS[c][1]], F32)
-            nc.vector.tensor_tensor(out=m[g, c][:], in0=s[g, c][:], in1=v[g][:, :, cols(c)], op=ALU.mult)
+            nc.vector.tensor_tensor(out=m[c][:, g], in0=s[c][:, g], in1=v[g][:, :, cols(c)], op=ALU.mult)
 
         def add(g, c):
-            nc.vector.tensor_tensor(out=y[g][:, :, cols(c)], in0=m[g, c][:], in1=u[g][:, :, cols(c)], op=ALU.add)
+            nc.vector.tensor_tensor(out=y[:, g, :, cols(c)], in0=m[c][:, g], in1=u[g][:, :, cols(c)], op=ALU.add)
 
-        def round_and_move(g, c):
-            pairs = new("pairs%d%d" % (g, c), [P, CHUNKS[c][1], PAIR], BF16)
-            nc.scalar.copy(out=pairs[:], in_=y[g][:, :, cols(c)].rearrange("q j n -> q n j"))
+        def round_y(gs, c, copy):
+            copy(out=pairs[c][:, gs], in_=y[:, gs, :, cols(c)].rearrange("q g j n -> q g n j"))
+
+        def move(g, c):
             nc.sync.dma_start(
                 out=moved[c][ROWS * g : ROWS * (g + 1), :, :],
-                in_=pairs[:].rearrange("q n j -> q (n j)").bitcast(F32),
+                in_=pairs[c][:, g].rearrange("q n j -> q (n j)").bitcast(F32),
             )
 
-        def store_y(g, columns):
-            rows = out_0[M * g : M * (g + 1), :].rearrange("(q j) n -> q j n", j=PAIR)
-            nc.sync.dma_start(out=rows[:, :, columns], in_=y[g][:, :, columns])
-
-        for g, c in pieces:
-            root(g, c)
+        both = slice(0, G)
+        for g in range(G):
+            root(slice(g, g + 1), 0)
+        for c in range(1, len(CHUNKS)):
+            root(both, c)
         scale_in(*pieces[0])
         for i, (g, c) in enumerate(pieces):
             if i + 1 < len(pieces):
                 scale_in(*pieces[i + 1])
             add(g, c)
-            round_and_move(g, c)
-            if i % len(CHUNKS) == len(CHUNKS) - 1:
-                store_y(g, slice(0, N))
+            if c == 0:
+                if g == 1:
+                    round_y(both, c, nc.scalar.copy)
+                    move(0, c)
+                    move(1, c)
+            else:
+                round_y(slice(g, g + 1), c, nc.scalar.copy)
+                move(g, c)
+        for g in range(G):
+            rows = out_0[M * g : M * (g + 1), :].rearrange("(q j) n -> q j n", j=PAIR)
+            nc.sync.dma_start(out=rows, in_=y[:, g])
 
         y_codes = new("y_codes", [P, N], U32)
         y_scales = new("y_scales", [P, N], U8)

from contextlib import ExitStack

import concourse.mybir as mybir

G, D, M, N = 2, 256, 256, 512
FLOPS = 2 * G * 2 * D * M * N

F32 = mybir.dt.float32
BF16 = mybir.dt.bfloat16
I32 = mybir.dt.int32
U32 = mybir.dt.uint32
U8 = mybir.dt.uint8
FP8X4 = mybir.dt.float8_e4m3fn_x4
ACT = mybir.ActivationFunctionType
ALU = mybir.AluOpType

P = 128
PACK = 4
ROWS = D // PACK
PAIR = M // P
HALF = N // 2
STEP = 128
H_SPLIT = 176
CHUNKS = [(0, 128), (128, 256), (384, 128)]


def tile_rows_pl_cell_rglru_kernel(tc, h, wr, wi, xh, hp, la, br, bi, out_0, out_1, out_2):
    nc = tc.nc
    with ExitStack() as ctx:
        sb = ctx.enter_context(tc.tile_pool(name="sb", bufs=1))
        psum = ctx.enter_context(tc.psum_pool(name="psum", bufs=1))
        ctx.enter_context(tc.manual_schedule())

        def new(name, shape, dtype):
            return sb.tile(shape, dtype, name=name, align_bytes=64)

        par = new("par", [P, G, 64], F32)
        nc.vector.memset(par[:], 0.0)

        def load_w(k, w):
            raw = new("w_raw%d" % k, [P, PACK, M], F32)
            nc.sync.dma_start(out=raw[:], in_=w.rearrange("g (p t) m -> (g p) t m", t=PACK))
            return raw

        def load_h(e):
            raw = new("h_raw%d" % e, [P, PACK, HALF], F32)
            nc.sync.dma_start(out=raw[:], in_=h.rearrange("g (p t) n -> (g p) t n", t=PACK)[:, :, HALF * e : HALF * (e + 1)])
            return raw

        h_raw = [load_h(0)]
        for k, vec in enumerate((br, la, bi)):
            nc.sync.dma_start(out=par[k:P:32, :, :], in_=vec.rearrange("g (b x) o -> b g (x o)", x=64))
        w_raw = [load_w(0, wr)]
        h_raw.append(load_h(1))
        w_raw.append(load_w(1, wi))
        hp_sb, xh_sb = [], []
        for name, src, dst in (("hp", hp, hp_sb), ("xh", xh, xh_sb)):
            for g in range(G):
                dst.append(new("%s%d" % (name, g), [P, PAIR, N], F32))
                nc.sync.dma_start(out=dst[g][:], in_=src[g].rearrange("(q j) n -> q j n", j=PAIR))

        def col(k, g, j):
            x = 32 * (PAIR * g + j) + k
            return half[:, x : x + 1]

        h_bf, h_codes, h_scales = {}, {}, {}

        def round_h(e, split):
            h_bf[e] = new("h_bf%d" % e, [P, HALF, PACK], BF16)
            h_in = h_raw[e][:].rearrange("p t (c i) -> p c t i", i=4)
            h_out = h_bf[e][:].rearrange("p (c i) t -> p c t i", i=4)
            nc.vector.tensor_copy(out=h_out[:, : split // 4], in_=h_in[:, : split // 4])
            if split < HALF:
                nc.scalar.copy(out=h_out[:, split // 4 :], in_=h_in[:, split // 4 :])

        def quant_h(e):
            h_codes[e] = new("h_codes%d" % e, [P, HALF], U32)
            h_scales[e] = new("h_scales%d" % e, [P, HALF], U8)
            nc.vector.quantize_mx(
                out=h_codes[e][:].bitcast(FP8X4), scales=h_scales[e][:], in_=h_bf[e][:].rearrange("p n t -> p (n t)")
            )

        w_bf = [new("w_bf%d" % k, [P, PAIR, P, PACK], BF16) for k in range(2)]
        w_codes = [new("w_codes%d" % k, [P, PAIR * P], U32) for k in range(2)]
        w_scales = [new("w_scales%d" % k, [P, PAIR * P], U8) for k in range(2)]

        def round_w(k, js, copy):
            copy(
                out=w_bf[k][:].rearrange("p j (c i) t -> p c t i j", i=2)[:, :, :, :, js],
                in_=w_raw[k][:].rearrange("p t (c i j) -> p c t i j", i=2, j=PAIR)[:, :, :, :, js],
            )

        def quant_w(k, js):
            part = slice(P * js.start, P * js.stop)
            nc.vector.quantize_mx(
                out=w_codes[k][:, part].bitcast(FP8X4),
                scales=w_scales[k][:, part],
                in_=w_bf[k][:, js].rearrange("p j q t -> p (j q t)"),
            )

        z = {}
        for k in range(2):
            for g in range(G):
                for j in range(PAIR):
                    z[k, g, j] = psum.tile([P, N], F32, name="z%d%d%d" % (k, g, j))

        def products(k, j, e):
            for n0 in range(0, HALF, STEP):
                for g in range(G):
                    rows = slice(ROWS * g, ROWS * (g + 1))
                    nc.tensor.matmul_mx(
                        out=z[k, g, j][:, HALF * e + n0 : HALF * e + n0 + STEP],
                        lhsT=w_codes[k][rows, P * j : P * (j + 1)].bitcast(FP8X4),
                        lhsT_scale=w_scales[k][rows, P * j : P * (j + 1)],
                        rhs=h_codes[e][rows, n0 : n0 + STEP].bitcast(FP8X4),
                        rhs_scale=h_scales[e][rows, n0 : n0 + STEP],
                        start=True,
                        stop=True,
                    )

        round_h(0, H_SPLIT)
        halved = new("halved", [P, G * PAIR * 32], F32)
        nc.scalar.activation(
            out=halved[:].rearrange("r (g j a) -> r g j a", g=G, j=PAIR),
            in_=par[:].rearrange("r g (a j) -> r g j a", j=PAIR),
            func=ACT.Copy,
            scale=0.5,
        )
        quant_h(0)
        half = new("half", [P, G * PAIR * 32], F32)
        nc.vector.transpose(out=half[:], in_=halved[:])
        round_w(0, slice(0, 1), nc.vector.tensor_copy)
        round_w(0, slice(1, 2), nc.scalar.copy)
        quant_w(0, slice(0, 1))
        quant_w(0, slice(1, 2))
        round_h(1, HALF)
        quant_h(1)
        round_w(1, slice(0, 2), nc.vector.tensor_copy)
        quant_w(1, slice(0, 2))

        tr, a, u, ti, v = [], [], [], [], []
        a2 = new("a2", [P, G, PAIR, N], F32)
        for g in range(G):
            tr.append(new("tr%d" % g, [P, PAIR, N], F32))
            a.append(new("a%d" % g, [P, PAIR, N], F32))
            u.append(new("u%d" % g, [P, PAIR, N], F32))

        def tanh_r(g, j, e):
            part = slice(HALF * e, HALF * (e + 1))
            nc.scalar.activation(out=tr[g][:, j, part], in_=z[0, g, j][:, part], func=ACT.Tanh, bias=col(0, g, j), scale=0.5)

        for j in range(PAIR):
            products(0, j, 0)
        for j in range(PAIR):
            for g in range(G):
                tanh_r(g, j, 0)
        for j in range(PAIR):
            products(0, j, 1)
        for j in range(PAIR):
            for e in range(2):
                products(1, j, e)
        for g in range(G):
            for j in range(PAIR):
                tanh_r(g, j, 1)
            for j in range(PAIR):
                nc.scalar.activation(out=a[g][:, j, :], in_=tr[g][:, j, :], func=ACT.Exp, bias=col(1, g, j), scale=col(1, g, j))
            for js in [slice(0, 1), slice(1, 2)] if g == 0 else [slice(0, 2)]:
                nc.vector.tensor_tensor(out=a2[:, g, js, :], in0=a[g][:, js, :], in1=a[g][:, js, :], op=ALU.mult)
                nc.vector.tensor_tensor(out=u[g][:, js, :], in0=a[g][:, js, :], in1=hp_sb[g][:, js, :], op=ALU.mult)
        for g in range(G):
            ti.append(new("ti%d" % g, [P, PAIR, N], F32))
            v.append(new("v%d" % g, [P, PAIR, N], F32))
            for j in range(PAIR):
                nc.scalar.activation(out=ti[g][:, j, :], in_=z[1, g, j][:], func=ACT.Tanh, bias=col(2, g, j), scale=0.5)
            nc.vector.scalar_tensor_tensor(out=v[g][:], in0=ti[g][:], scalar=1.0, in1=xh_sb[g][:], op0=ALU.add, op1=ALU.mult)

        pieces = [(g, c) for c in range(len(CHUNKS)) for g in range(G)]
        y = new("y", [P, G, PAIR, N], F32)
        s, m, pairs, moved = [], [], [], []
        for c, (n0, w) in enumerate(CHUNKS):
            s.append(new("s%d" % c, [P, G, PAIR, w], F32))
            m.append(new("m%d" % c, [P, G, PAIR, w], F32))
            pairs.append(new("pairs%d" % c, [P, G, w, PAIR], BF16))
            moved.append(new("moved%d" % c, [P, 2, w], F32))

        def cols(c):
            return slice(CHUNKS[c][0], CHUNKS[c][0] + CHUNKS[c][1])

        def root(gs, c):
            nc.scalar.activation(out=s[c][:, gs], in_=a2[:, gs, :, cols(c)], func=ACT.Sqrt, bias=0.25, scale=-0.25)

        def scale_in(g, c):
            nc.vector.tensor_tensor(out=m[c][:, g], in0=s[c][:, g], in1=v[g][:, :, cols(c)], op=ALU.mult)

        def add(g, c):
            nc.vector.tensor_tensor(out=y[:, g, :, cols(c)], in0=m[c][:, g], in1=u[g][:, :, cols(c)], op=ALU.add)

        def round_y(gs, c, copy):
            copy(out=pairs[c][:, gs], in_=y[:, gs, :, cols(c)].rearrange("q g j n -> q g n j"))

        def move(g, c):
            nc.sync.dma_start(
                out=moved[c][ROWS * g : ROWS * (g + 1), :, :],
                in_=pairs[c][:, g].rearrange("q n j -> q (n j)").bitcast(F32),
            )

        both = slice(0, G)
        for g in range(G):
            root(slice(g, g + 1), 0)
        for c in range(1, len(CHUNKS)):
            root(both, c)
        scale_in(*pieces[0])
        for i, (g, c) in enumerate(pieces):
            if i + 1 < len(pieces):
                scale_in(*pieces[i + 1])
            add(g, c)
            if c == 0:
                if g == 1:
                    round_y(both, c, nc.scalar.copy)
                    move(0, c)
                    move(1, c)
            else:
                round_y(slice(g, g + 1), c, nc.scalar.copy)
                move(g, c)
        for g in range(G):
            rows = out_0[M * g : M * (g + 1), :].rearrange("(q j) n -> q j n", j=PAIR)
            nc.sync.dma_start(out=rows, in_=y[:, g])

        y_codes = new("y_codes", [P, N], U32)
        y_scales = new("y_scales", [P, N], U8)
        words = out_1[0].rearrange("p n t -> p (n t)").bitcast(I32)
        for c, (n0, w) in enumerate(CHUNKS):
            y_bf = new("y_bf%d" % c, [P, w * PACK], BF16)
            nc.vector.tensor_copy(
                out=y_bf[:].bitcast(F32).rearrange("p (n a) -> p n a", a=2),
                in_=moved[c][:].rearrange("p a n -> p n a"),
            )
            nc.vector.quantize_mx(out=y_codes[:, cols(c)].bitcast(FP8X4), scales=y_scales[:, cols(c)], in_=y_bf[:])
            nc.sync.dma_start(out=words[:, cols(c)], in_=y_codes[:, cols(c)].bitcast(I32))
        for q in range(4):
            queue = nc.scalar if q % 2 else nc.sync
            queue.dma_start(out=out_2[0, 4 * q : 4 * q + 4, :].bitcast(I32), in_=y_scales[32 * q : 32 * q + 4, :].bitcast(I32))
